import numpy as np
import ml_dtypes


def mxq(x, axis, fmt="e4m3"):
    dtype, down = {"e4m3": (ml_dtypes.float8_e4m3fn, 7), "e5m2": (ml_dtypes.float8_e5m2, 14)}[fmt]
    v = np.moveaxis(np.asarray(x, np.float32).astype(ml_dtypes.bfloat16).astype(np.float64), axis, -1)
    blocks = v.reshape(v.shape[:-1] + (-1, 32))
    amax = np.abs(blocks).max(-1, keepdims=True)
    byte = np.maximum(np.where(amax > 0, np.frexp(amax)[1] - 1 + 127, 0) - down, 1)
    scale = np.exp2(byte - 127.0)
    codes = (blocks / scale).astype(np.float32).astype(dtype).astype(np.float64)
    return np.moveaxis((codes * scale).reshape(v.shape), -1, axis)


WIDE = False


def mx_kscale(k):
    if not WIDE:
        return np.ones(k)
    levels = np.array([10, -10, 5, -5, 0])
    if k % 512:
        return np.exp2(np.random.permutation(np.resize(levels, k // 32))).repeat(32)
    a = np.empty((k // 512, 16))
    for p in range(k // 512):
        a[p, :8] = np.random.permutation(np.resize(levels, 8))
        for g in range(8):
            far = levels[np.abs(levels - a[p, g]) >= 10]
            a[p, g + 8] = far[np.random.randint(len(far))]
    return np.exp2(a.ravel()).repeat(32)


def f64(x):
    return np.asarray(x).astype(np.float64)


def striped(idx):
    return np.tile(idx.reshape(-1, 16).T, (8, 1)).astype(np.uint16)


def unstriped(offs):
    return offs[:16].T.reshape(-1).astype(np.int64)


def pack_weight(w):
    k, n = w.shape
    w = f64(np.asarray(w, np.float32).astype(ml_dtypes.bfloat16)).reshape(k // 32, 32, n)
    amax = np.abs(w).max(1)
    byte = np.clip(np.where(amax > 0, np.frexp(amax)[1] - 1 + 127 - 7, 1), 1, 254)
    scaled = (w * np.exp2(127.0 - byte)[:, None, :]).reshape(k, n).astype(np.float32)
    words = np.ascontiguousarray(scaled.reshape(k // 512, 128, 4, n).transpose(0, 1, 3, 2)).astype(ml_dtypes.float8_e4m3fn).view(np.uint8)
    return words, np.ascontiguousarray(byte.astype(np.uint8).reshape(k // 512, 16, n))


def unpack_weight(words, scales):
    g, p, n, _ = words.shape
    vals = np.ascontiguousarray(words).view(ml_dtypes.float8_e4m3fn).astype(np.float64) * np.repeat(np.exp2(scales.astype(np.float64) - 127.0), 8, axis=1)[..., None]
    return vals.transpose(0, 1, 3, 2).reshape(g * 512, n)


def relu(v):
    return np.maximum(v, 0.0)


K, T, D, S, V, R, N = 512, 4096, 3, 3072, 1024, 4, 512


def setup_inputs():
    n = np.random.standard_normal
    s = mx_kscale(K)[:, None]
    packed = pack_weight(n((K, T)) * s)
    return {
        "x_words": packed[0],
        "x_scales": packed[1],
        "w": (n((D, K, N)) / np.sqrt(D * K) / s[None]).astype(np.float32),
        "b": (0.3 * n((N, 1))).astype(np.float32),
        "offs": striped(np.concatenate([R * np.arange(V) + np.random.randint(0, R, V) for _ in range(D)])),
    }


def reference(x_words, x_scales, w, b, offs):
    idx = unstriped(offs)
    xq = unpack_weight(x_words, x_scales)[:, idx]
    wq = mxq(f64(w), 1, "e4m3")
    y = sum(wq[d].T @ xq[:, d * V:(d + 1) * V] for d in range(D))
    y = relu(y + f64(b))
    return y

@@ -1,0 +1,182 @@
+from contextlib import ExitStack
+
+import concourse.mybir as mybir
+
+K, T, D, V, R, N = 512, 4096, 3, 1024, 4, 512
+FLOPS = 2 * K * N * D * V
+
+F32 = mybir.dt.float32
+BF16 = mybir.dt.bfloat16
+I32 = mybir.dt.int32
+U32 = mybir.dt.uint32
+U16 = mybir.dt.uint16
+U8 = mybir.dt.uint8
+FP8X4 = mybir.dt.float8_e4m3fn_x4
+RELU = mybir.ActivationFunctionType.Relu
+ADD = mybir.AluOpType.add
+MAX = mybir.AluOpType.max
+
+P = 128
+PACK = 4
+HALF = N // 2
+
+
+def tile_picked_deform_lin_relu_def_p_kernel(tc, x_words, x_scales, w, b, offs, out):
+    nc = tc.nc
+    with ExitStack() as ctx:
+        keep = ctx.enter_context(tc.tile_pool(name="keep", bufs=1))
+        psum = ctx.enter_context(tc.psum_pool(name="psum", bufs=1))
+
+        offsets = keep.tile([P, D * V // 16], U16, name="offsets")
+        nc.sync.dma_start(offsets[:], offs)
+
+        def entries(d, v0, v1):
+            return offsets[:, (d * V + v0) // 16:(d * V + v1) // 16]
+
+        scale_table = keep.tile([P, T // 4], I32, name="scale_table", align_bytes=64)
+        nc.vector.memset(scale_table[:], 0)
+        zero = keep.tile([P, 1], F32, name="zero")
+        nc.vector.memset(zero[:], 0.0)
+        floor = keep.tile([P, 1], F32, name="floor")
+        nc.scalar.activation(floor[:], zero[:], RELU)
+        bias = keep.tile([P, N // P], F32, name="bias")
+        with nc.allow_non_contiguous_dma(reason="one bias value a partition"):
+            nc.scalar.dma_start(bias[:], b.rearrange("(c p) o -> p (c o)", p=P))
+
+        words_hbm = x_words[0].rearrange("p c r -> p (c r)")
+        tables = {
+            "high": keep.tile([P, T], I32, name="table_high", align_bytes=64),
+            "mid": keep.tile([P, T // 2], I32, name="table_mid", align_bytes=64),
+            "low": keep.tile([P, T // 8], I32, name="table_low", align_bytes=64),
+        }
+        chunks = {"first": ("mid", 128, 256), "high": ("high", 512, 1024), "mid": ("mid", 256, 512), "last": ("low", 0, 128)}
+
+        def load_words(chunk):
+            table, v0, v1 = chunks[chunk]
+            nc.sync.dma_start(tables[table][:, R * v0:R * v1], words_hbm[:, 4 * R * v0:4 * R * v1].bitcast(I32))
+
+        picked = {}
+
+        def gather_words(chunk, d):
+            table, v0, v1 = chunks[chunk]
+            got = keep.tile([P, v1 - v0], U32, name=f"words_{chunk}_{d}", align_bytes=64)
+            nc.vector.tensor_copy(got[:], tables[table][:, 0:R * v1].bitcast(U32).indirect(entries(d, v0, v1)))
+            picked[chunk, d] = got
+
+        picked_scales = {}
+
+        def gather_scales(vh, d):
+            got = keep.tile([P, V // 2], U8, name=f"scales_{vh}_{d}", align_bytes=64)
+            v0, v1 = vh * V // 2, (vh + 1) * V // 2
+            nc.vector.tensor_copy(got[:], scale_table[:, 0:v1].bitcast(U8).indirect(entries(d, v0, v1)))
+            picked_scales[vh, d] = got
+
+        raw, grouped, w_codes, w_scales = {}, {}, {}, {}
+
+        def load_w(h, d):
+            raw[h, d] = keep.tile([P, PACK, HALF], F32, name=f"raw_{h}_{d}", align_bytes=64)
+            nc.sync.dma_start(raw[h, d][:], w[d].rearrange("(p t) m -> p t m", t=PACK)[:, :, h * HALF:(h + 1) * HALF])
+
+        def round_w(h, d):
+            grouped[h, d] = keep.tile([P, HALF, PACK], BF16, name=f"grouped_{h}_{d}", align_bytes=64)
+            nc.scalar.copy(grouped[h, d][:].rearrange("p (c i) t -> p c t i", i=4),
+                           raw[h, d][:].rearrange("p t (c i) -> p c t i", i=4))
+
+        def quantize_w(h, d):
+            w_codes[h, d] = keep.tile([P, HALF], U32, name=f"w_codes_{h}_{d}", align_bytes=64)
+            w_scales[h, d] = keep.tile([P, HALF], U8, name=f"w_scales_{h}_{d}", align_bytes=64)
+            nc.vector.quantize_mx(out=w_codes[h, d][:].bitcast(FP8X4), scales=w_scales[h, d][:],
+                                  in_=grouped[h, d][:].rearrange("p m t -> p (m t)"))
+
+        def multiply(acc, c, chunk, d):
+            h, m0 = c // 2, (c % 2) * P
+            v0, v1 = chunks[chunk][1:]
+            vh = v0 // (V // 2)
+            s0 = v0 - vh * (V // 2)
+            nc.tensor.matmul_mx(out=acc, lhsT=w_codes[h, d][:, m0:m0 + P].bitcast(FP8X4), lhsT_scale=w_scales[h, d][:, m0:m0 + P],
+                                rhs=picked[chunk, d][:].bitcast(FP8X4), rhs_scale=picked_scales[vh, d][:, s0:s0 + v1 - v0],
+                                start=(d == 0), stop=(d == D - 1))
+
+        def finish(dst, acc, c, on_vector):
+            if on_vector:
+                nc.vector.tensor_scalar(dst, acc, bias[:, c:c + 1], floor[:], ADD, MAX)
+            else:
+                nc.scalar.activation(dst, acc, RELU, bias=bias[:, c:c + 1])
+
+        out_rows = out.rearrange("(c p) v -> p c v", p=P)
+
+        load_words("first")
+        for q in range(4):
+            nc.sync.dma_start(scale_table[32 * q:32 * q + 4, :], x_scales[0][4 * q:4 * q + 4, :].bitcast(I32))
+        load_w(0, 0)
+        load_w(0, 1)
+        load_words("high")
+        load_w(0, 2)
+        for d in range(D):
+            load_w(1, d)
+        load_words("mid")
+        load_words("last")
+
+        for h in range(2):
+            for d in range(D):
+                if (h, d) < (1, 0):
+                    round_w(h, d)
+        for d in range(D):
+            gather_words("first", d)
+        for vh in (1, 0):
+            for d in range(D):
+                gather_scales(vh, d)
+        quantize_w(0, 0)
+        quantize_w(0, 1)
+        for d in range(D):
+            gather_words("high", d)
+        quantize_w(0, 2)
+
+        high = [psum.tile([P, 512], F32, name=f"high_{c}", tag=f"bank{c}") for c in range(4)]
+        lower = [psum.tile([P, 512], F32, name=f"lower_{c}", tag=f"bank{4 + c}") for c in range(4)]
+
+        def high_and_first(h):
+            for d in range(D):
+                for c in (2 * h, 2 * h + 1):
+                    multiply(high[c][:], c, "high", d)
+            for d in range(D):
+                for c in (2 * h, 2 * h + 1):
+                    multiply(lower[c][:, 0:128], c, "first", d)
+
+        def store_high(h):
+            res = keep.tile([P, 2, 512], F32, name=f"res_high_{h}")
+            for j in range(2):
+                finish(res[:, j, :], high[2 * h + j][:], 2 * h + j, False)
+            nc.sync.dma_start(out_rows[:, 2 * h:2 * h + 2, 512:1024], res[:])
+
+        high_and_first(0)
+        round_w(1, 0)
+        round_w(1, 1)
+        store_high(0)
+        round_w(1, 2)
+        for d in range(D):
+            quantize_w(1, d)
+        high_and_first(1)
+        store_high(1)
+
+        for d in range(D):
+            gather_words("mid", d)
+        for d in range(D):
+            for c in range(4):
+                multiply(lower[c][:, 128:384], c, "mid", d)
+        for d in range(D):
+            gather_words("last", d)
+        for h in range(2):
+            res = keep.tile([P, 2, 384], F32, name=f"res_mid_{h}")
+            for j in range(2):
+                finish(res[:, j, :], lower[2 * h + j][:, 0:384], 2 * h + j, False)
+            nc.sync.dma_start(out_rows[:, 2 * h:2 * h + 2, 128:512], res[:])
+
+        last = [psum.tile([P, 512], F32, name=f"last_{c}", tag=f"bank{c}") for c in range(4)]
+        for d in range(D):
+            for c in range(4):
+                multiply(last[c][:, 0:128], c, "last", d)
+        res_last = keep.tile([P, 4, 128], F32, name="res_last")
+        for c in range(4):
+            finish(res_last[:, c, :], last[c][:, 0:128], c, True)
+        nc.sync.dma_start(out_rows[:, :, 0:128], res_last[:])

@@ -35,6 +35,8 @@ def tile_picked_deform_lin_relu_def_p_kernel(tc, x_words, x_scales, w, b, offs, 
 
         scale_table = keep.tile([P, T // 4], I32, name="scale_table", align_bytes=64)
         nc.vector.memset(scale_table[:], 0)
+        for q in range(4):
+            nc.scalar.dma_start(scale_table[32 * q:32 * q + 4, :], x_scales[0][4 * q:4 * q + 4, :].bitcast(I32))
         zero = keep.tile([P, 1], F32, name="zero")
         nc.vector.memset(zero[:], 0.0)
         floor = keep.tile([P, 1], F32, name="floor")
@@ -106,11 +108,9 @@ def tile_picked_deform_lin_relu_def_p_kernel(tc, x_words, x_scales, w, b, offs, 
         out_rows = out.rearrange("(c p) v -> p c v", p=P)
 
         load_words("first")
-        for q in range(4):
-            nc.sync.dma_start(scale_table[32 * q:32 * q + 4, :], x_scales[0][4 * q:4 * q + 4, :].bitcast(I32))
         load_w(0, 0)
-        load_w(0, 1)
         load_words("high")
+        load_w(0, 1)
         load_w(0, 2)
         for d in range(D):
             load_w(1, d)
@@ -123,14 +123,15 @@ def tile_picked_deform_lin_relu_def_p_kernel(tc, x_words, x_scales, w, b, offs, 
                     round_w(h, d)
         for d in range(D):
             gather_words("first", d)
-        for vh in (1, 0):
-            for d in range(D):
-                gather_scales(vh, d)
+        for d in range(D):
+            gather_scales(1, d)
         quantize_w(0, 0)
-        quantize_w(0, 1)
         for d in range(D):
             gather_words("high", d)
+        quantize_w(0, 1)
         quantize_w(0, 2)
+        for d in range(D):
+            gather_scales(0, d)
 
         high = [psum.tile([P, 512], F32, name=f"high_{c}", tag=f"bank{c}") for c in range(4)]
         lower = [psum.tile([P, 512], F32, name=f"lower_{c}", tag=f"bank{4 + c}") for c in range(4)]
@@ -149,14 +150,19 @@ def tile_picked_deform_lin_relu_def_p_kernel(tc, x_words, x_scales, w, b, offs, 
                 finish(res[:, j, :], high[2 * h + j][:], 2 * h + j, False)
             nc.sync.dma_start(out_rows[:, 2 * h:2 * h + 2, 512:1024], res[:])
 
+        res_first = keep.tile([P, 4, 128], F32, name="res_first")
         high_and_first(0)
-        round_w(1, 0)
-        round_w(1, 1)
+        for d in range(D):
+            round_w(1, d)
         store_high(0)
-        round_w(1, 2)
+        for c in range(2):
+            finish(res_first[:, c, :], lower[c][:, 0:128], c, False)
         for d in range(D):
             quantize_w(1, d)
         high_and_first(1)
+        for c in range(2, 4):
+            finish(res_first[:, c, :], lower[c][:, 0:128], c, False)
+        nc.sync.dma_start(out_rows[:, :, 128:256], res_first[:])
         store_high(1)
 
         for d in range(D):
@@ -167,10 +173,10 @@ def tile_picked_deform_lin_relu_def_p_kernel(tc, x_words, x_scales, w, b, offs, 
         for d in range(D):
             gather_words("last", d)
         for h in range(2):
-            res = keep.tile([P, 2, 384], F32, name=f"res_mid_{h}")
+            res = keep.tile([P, 2, 256], F32, name=f"res_mid_{h}")
             for j in range(2):
-                finish(res[:, j, :], lower[2 * h + j][:, 0:384], 2 * h + j, False)
-            nc.sync.dma_start(out_rows[:, 2 * h:2 * h + 2, 128:512], res[:])
+                finish(res[:, j, :], lower[2 * h + j][:, 128:384], 2 * h + j, False)
+            nc.sync.dma_start(out_rows[:, 2 * h:2 * h + 2, 256:512], res[:])
 
         last = [psum.tile([P, 512], F32, name=f"last_{c}", tag=f"bank{c}") for c in range(4)]
         for d in range(D):

@@ -33,56 +33,67 @@ def tile_picked_deform_lin_relu_def_p_kernel(tc, x_words, x_scales, w, b, offs, 
         def entries(d, v0, v1):
             return offsets[:, (d * V + v0) // 16:(d * V + v1) // 16]
 
-        scale_table = keep.tile([P, T // 4], I32, name="scale_table", align_bytes=64)
+        scale_table = keep.tile([P, T // 4], I32, name="scale_table", tag="scale_table", align_bytes=64)
         nc.vector.memset(scale_table[:], 0)
-        for q in range(4):
-            nc.scalar.dma_start(scale_table[32 * q:32 * q + 4, :], x_scales[0][4 * q:4 * q + 4, :].bitcast(I32))
-        zero = keep.tile([P, 1], F32, name="zero")
-        nc.vector.memset(zero[:], 0.0)
         floor = keep.tile([P, 1], F32, name="floor")
-        nc.scalar.activation(floor[:], zero[:], RELU)
-        bias = keep.tile([P, N // P], F32, name="bias")
-        with nc.allow_non_contiguous_dma(reason="one bias value a partition"):
-            nc.scalar.dma_start(bias[:], b.rearrange("(c p) o -> p (c o)", p=P))
+        with tc.tile_pool(name="head", bufs=1) as head:
+            zero = head.tile([P, 16384], F32, name="zero")
+            nc.vector.memset(zero[:, 0:1], 0.0)
+            nc.scalar.activation(floor[:], zero[:, 0:1], RELU)
+        later = ctx.enter_context(tc.tile_pool(name="later", bufs=1))
+        bias = later.tile([P, N // P], F32, name="bias")
 
         words_hbm = x_words[0].rearrange("p c r -> p (c r)")
         tables = {
-            "high": keep.tile([P, T], I32, name="table_high", align_bytes=64),
-            "mid": keep.tile([P, T // 2], I32, name="table_mid", align_bytes=64),
-            "low": keep.tile([P, T // 8], I32, name="table_low", align_bytes=64),
+            "high": later.tile([P, T], I32, name="table_high", tag="table_high", align_bytes=64),
+            "mid": later.tile([P, T // 2], I32, name="table_mid", align_bytes=64),
+            "first": keep.tile([P, T // 4], I32, name="table_first", align_bytes=64),
+            "low": later.tile([P, T // 8], I32, name="table_low", align_bytes=64),
         }
-        chunks = {"first": ("mid", 128, 256), "high": ("high", 512, 1024), "mid": ("mid", 256, 512), "last": ("low", 0, 128)}
+        chunks = {"first": ("first", 128, 256), "high": ("high", 512, 1024), "mid": ("mid", 256, 512), "last": ("low", 0, 128)}
 
         def load_words(chunk):
             table, v0, v1 = chunks[chunk]
             nc.sync.dma_start(tables[table][:, R * v0:R * v1], words_hbm[:, 4 * R * v0:4 * R * v1].bitcast(I32))
 
-        picked = {}
+        picked, narrow = {}, {}
 
         def gather_words(chunk, d):
             table, v0, v1 = chunks[chunk]
-            got = keep.tile([P, v1 - v0], U32, name=f"words_{chunk}_{d}", align_bytes=64)
-            nc.vector.tensor_copy(got[:], tables[table][:, 0:R * v1].bitcast(U32).indirect(entries(d, v0, v1)))
+            if chunk == "first":
+                got = keep.tile([P, P], U32, name=f"words_first_{d}", align_bytes=64)[:]
+            elif chunk == "last":
+                got = narrow["end"][:, 768 + d * P:768 + (d + 1) * P]
+            elif chunk == "mid":
+                if d == 0:
+                    narrow["end"] = keep.tile([P, 768 + D * P], U32, name="words_end", tag="scale_table", align_bytes=64)
+                got = narrow["end"][:, 256 * d:256 * (d + 1)]
+            else:
+                got = keep.tile([P, v1 - v0], U32, name=f"words_{chunk}_{d}", align_bytes=64)[:]
+            nc.vector.tensor_copy(got, tables[table][:, 0:R * v1].bitcast(U32).indirect(entries(d, v0, v1)))
             picked[chunk, d] = got
 
         picked_scales = {}
 
         def gather_scales(vh, d):
-            got = keep.tile([P, V // 2], U8, name=f"scales_{vh}_{d}", align_bytes=64)
+            if vh == 1 or d == 0:
+                got = keep.tile([P, V // 2], U8, name=f"scales_{vh}_{d}", align_bytes=64)[:]
+            else:
+                got = keep.tile([P, V // 2], U8, name=f"scales_{vh}_{d}", tag=f"stage_1_{d}", align_bytes=64)[:]
             v0, v1 = vh * V // 2, (vh + 1) * V // 2
-            nc.vector.tensor_copy(got[:], scale_table[:, 0:v1].bitcast(U8).indirect(entries(d, v0, v1)))
+            nc.vector.tensor_copy(got, scale_table[:, 0:v1].bitcast(U8).indirect(entries(d, v0, v1)))
             picked_scales[vh, d] = got
 
         raw, grouped, w_codes, w_scales = {}, {}, {}, {}
 
         def load_w(h, d):
-            raw[h, d] = keep.tile([P, PACK, HALF], F32, name=f"raw_{h}_{d}", align_bytes=64)
+            raw[h, d] = later.tile([P, PACK, HALF], F32, name=f"raw_{h}_{d}", tag=f"wide_{h}_{d}", align_bytes=64)
             nc.sync.dma_start(raw[h, d][:], w[d].rearrange("(p t) m -> p t m", t=PACK)[:, :, h * HALF:(h + 1) * HALF])
 
         def round_w(h, d):
-            grouped[h, d] = keep.tile([P, HALF, PACK], BF16, name=f"grouped_{h}_{d}", align_bytes=64)
-            nc.scalar.copy(grouped[h, d][:].rearrange("p (c i) t -> p c t i", i=4),
-                           raw[h, d][:].rearrange("p t (c i) -> p c t i", i=4))
+            grouped[h, d] = keep.tile([P, HALF, PACK], BF16, name=f"grouped_{h}_{d}", tag=f"stage_{h}_{d}", align_bytes=64)
+            nc.scalar.copy(grouped[h, d][:].rearrange("p (c i) t -> p c t i", i=2),
+                           raw[h, d][:].rearrange("p t (c i) -> p c t i", i=2))
 
         def quantize_w(h, d):
             w_codes[h, d] = keep.tile([P, HALF], U32, name=f"w_codes_{h}_{d}", align_bytes=64)
@@ -96,7 +107,7 @@ def tile_picked_deform_lin_relu_def_p_kernel(tc, x_words, x_scales, w, b, offs, 
             vh = v0 // (V // 2)
             s0 = v0 - vh * (V // 2)
             nc.tensor.matmul_mx(out=acc, lhsT=w_codes[h, d][:, m0:m0 + P].bitcast(FP8X4), lhsT_scale=w_scales[h, d][:, m0:m0 + P],
-                                rhs=picked[chunk, d][:].bitcast(FP8X4), rhs_scale=picked_scales[vh, d][:, s0:s0 + v1 - v0],
+                                rhs=picked[chunk, d].bitcast(FP8X4), rhs_scale=picked_scales[vh, d][:, s0:s0 + v1 - v0],
                                 start=(d == 0), stop=(d == D - 1))
 
         def finish(dst, acc, c, on_vector):
@@ -108,12 +119,17 @@ def tile_picked_deform_lin_relu_def_p_kernel(tc, x_words, x_scales, w, b, offs, 
         out_rows = out.rearrange("(c p) v -> p c v", p=P)
 
         load_words("first")
+        for q in range(4):
+            nc.sync.dma_start(scale_table[32 * q:32 * q + 4, :], x_scales[0][4 * q:4 * q + 4, :].bitcast(I32))
         load_w(0, 0)
         load_words("high")
         load_w(0, 1)
         load_w(0, 2)
-        for d in range(D):
-            load_w(1, d)
+        load_w(1, 0)
+        with nc.allow_non_contiguous_dma(reason="one bias value a partition"):
+            nc.sync.dma_start(bias[:], b.rearrange("(c p) o -> p (c o)", p=P))
+        load_w(1, 1)
+        load_w(1, 2)
         load_words("mid")
         load_words("last")
 
@@ -125,57 +141,58 @@ def tile_picked_deform_lin_relu_def_p_kernel(tc, x_words, x_scales, w, b, offs, 
             gather_words("first", d)
         for d in range(D):
             gather_scales(1, d)
-        quantize_w(0, 0)
         for d in range(D):
+            quantize_w(0, d)
             gather_words("high", d)
-        quantize_w(0, 1)
-        quantize_w(0, 2)
         for d in range(D):
-            gather_scales(0, d)
+            round_w(1, d)
+        gather_scales(0, 0)
+        quantize_w(1, 0)
+        quantize_w(1, 1)
+        gather_scales(0, 1)
+        quantize_w(1, 2)
+        gather_scales(0, 2)
 
         high = [psum.tile([P, 512], F32, name=f"high_{c}", tag=f"bank{c}") for c in range(4)]
         lower = [psum.tile([P, 512], F32, name=f"lower_{c}", tag=f"bank{4 + c}") for c in range(4)]
 
-        def high_and_first(h):
+        def multiply_high(h):
             for d in range(D):
                 for c in (2 * h, 2 * h + 1):
                     multiply(high[c][:], c, "high", d)
-            for d in range(D):
-                for c in (2 * h, 2 * h + 1):
-                    multiply(lower[c][:, 0:128], c, "first", d)
 
         def store_high(h):
-            res = keep.tile([P, 2, 512], F32, name=f"res_high_{h}")
+            res = res_high[h]
             for j in range(2):
                 finish(res[:, j, :], high[2 * h + j][:], 2 * h + j, False)
-            nc.sync.dma_start(out_rows[:, 2 * h:2 * h + 2, 512:1024], res[:])
+            nc.sync.dma_start(out_rows[:, 2 * h:2 * h + 2, 512:1024], res)
 
-        res_first = keep.tile([P, 4, 128], F32, name="res_first")
-        high_and_first(0)
-        for d in range(D):
-            round_w(1, d)
-        store_high(0)
-        for c in range(2):
-            finish(res_first[:, c, :], lower[c][:, 0:128], c, False)
-        for d in range(D):
-            quantize_w(1, d)
-        high_and_first(1)
-        for c in range(2, 4):
-            finish(res_first[:, c, :], lower[c][:, 0:128], c, False)
-        nc.sync.dma_start(out_rows[:, :, 128:256], res_first[:])
-        store_high(1)
+        early = later.tile([P, 2 * 512 + 4 * 128], F32, name="res_early", tag="wide_1_2", align_bytes=64)
+        res_first = early[:, 1024:].rearrange("p (c v) -> p c v", c=4)
+        res_high = [early[:, 0:1024].rearrange("p (c v) -> p c v", c=2), keep.tile([P, 2, 512], F32, name="res_high_1")[:]]
+        for h in range(2):
+            multiply_high(h)
+            store_high(h)
+        first = [psum.tile([P, 512], F32, name=f"first_{h}", tag=f"bank{h}") for h in range(2)]
+        for j in range(2):
+            for d in range(D):
+                for h in range(2):
+                    multiply(first[h][:, j * P:(j + 1) * P], 2 * h + j, "first", d)
+        for c in range(4):
+            finish(res_first[:, c, :], first[c // 2][:, (c % 2) * P:(c % 2 + 1) * P], c, False)
+        nc.sync.dma_start(out_rows[:, :, 128:256], res_first)
 
         for d in range(D):
             gather_words("mid", d)
         for d in range(D):
             for c in range(4):
-                multiply(lower[c][:, 128:384], c, "mid", d)
+                multiply(lower[c][:, 0:256], c, "mid", d)
         for d in range(D):
             gather_words("last", d)
         for h in range(2):
             res = keep.tile([P, 2, 256], F32, name=f"res_mid_{h}")
             for j in range(2):
-                finish(res[:, j, :], lower[2 * h + j][:, 128:384], 2 * h + j, False)
+                finish(res[:, j, :], lower[2 * h + j][:, 0:256], 2 * h + j, False)
             nc.sync.dma_start(out_rows[:, 2 * h:2 * h + 2, 256:512], res[:])
 
         last = [psum.tile([P, 512], F32, name=f"last_{c}", tag=f"bank{c}") for c in range(4)]
@@ -185,4 +202,5 @@ def tile_picked_deform_lin_relu_def_p_kernel(tc, x_words, x_scales, w, b, offs, 
         res_last = keep.tile([P, 4, 128], F32, name="res_last")
         for c in range(4):
             finish(res_last[:, c, :], last[c][:, 0:128], c, True)
-        nc.sync.dma_start(out_rows[:, :, 0:128], res_last[:])
+            if c % 2:
+                nc.sync.dma_start(out_rows[:, c - 1:c + 1, 0:128], res_last[:, c - 1:c + 1, :])

@@ -2,8 +2,8 @@ from contextlib import ExitStack
 
 import concourse.mybir as mybir
 
-K, T, D, V, R, N = 512, 4096, 3, 1024, 4, 512
-FLOPS = 2 * K * N * D * V
+K, T, TAPS, V, STRIDE, M = 512, 4096, 3, 1024, 4, 512
+FLOPS = 2 * K * M * TAPS * V
 
 F32 = mybir.dt.float32
 BF16 = mybir.dt.bfloat16
@@ -18,7 +18,14 @@ MAX = mybir.AluOpType.max
 
 P = 128
 PACK = 4
-HALF = N // 2
+BLOCKS = M // P
+M_HALF = M // 2
+V_HALF = V // 2
+BANK = 512
+QUADRANT = 32
+HEAD_WORDS = 16384
+
+SPANS = {"first": (128, 256), "high": (512, 1024), "mid": (256, 512), "last": (0, 128)}
 
 
 def tile_picked_deform_lin_relu_def_p_kernel(tc, x_words, x_scales, w, b, offs, out):
@@ -27,180 +34,165 @@ def tile_picked_deform_lin_relu_def_p_kernel(tc, x_words, x_scales, w, b, offs, 
         keep = ctx.enter_context(tc.tile_pool(name="keep", bufs=1))
         psum = ctx.enter_context(tc.psum_pool(name="psum", bufs=1))
 
-        offsets = keep.tile([P, D * V // 16], U16, name="offsets")
+        offsets = keep.tile([P, TAPS * V // 16], U16, name="offsets")
         nc.sync.dma_start(offsets[:], offs)
 
         def entries(d, v0, v1):
             return offsets[:, (d * V + v0) // 16:(d * V + v1) // 16]
 
-        scale_table = keep.tile([P, T // 4], I32, name="scale_table", tag="scale_table", align_bytes=64)
+        scale_table = keep.tile([P, T // PACK], I32, name="scale_table", align_bytes=64)
         nc.vector.memset(scale_table[:], 0)
+
         floor = keep.tile([P, 1], F32, name="floor")
         with tc.tile_pool(name="head", bufs=1) as head:
-            zero = head.tile([P, 16384], F32, name="zero")
+            zero = head.tile([P, HEAD_WORDS], F32, name="zero")
             nc.vector.memset(zero[:, 0:1], 0.0)
             nc.scalar.activation(floor[:], zero[:, 0:1], RELU)
         later = ctx.enter_context(tc.tile_pool(name="later", bufs=1))
-        bias = later.tile([P, N // P], F32, name="bias")
+        bias = later.tile([P, BLOCKS], F32, name="bias")
 
         words_hbm = x_words[0].rearrange("p c r -> p (c r)")
-        tables = {
-            "high": later.tile([P, T], I32, name="table_high", tag="table_high", align_bytes=64),
-            "mid": later.tile([P, T // 2], I32, name="table_mid", align_bytes=64),
-            "first": keep.tile([P, T // 4], I32, name="table_first", align_bytes=64),
-            "low": later.tile([P, T // 8], I32, name="table_low", align_bytes=64),
-        }
-        chunks = {"first": ("first", 128, 256), "high": ("high", 512, 1024), "mid": ("mid", 256, 512), "last": ("low", 0, 128)}
+        tables = {}
+        for span in ("high", "mid", "first", "last"):
+            pool = keep if span == "first" else later
+            tables[span] = pool.tile([P, STRIDE * SPANS[span][1]], I32, name=f"table_{span}", align_bytes=64)
 
-        def load_words(chunk):
-            table, v0, v1 = chunks[chunk]
-            nc.sync.dma_start(tables[table][:, R * v0:R * v1], words_hbm[:, 4 * R * v0:4 * R * v1].bitcast(I32))
+        def load_words(span):
+            c0, c1 = STRIDE * SPANS[span][0], STRIDE * SPANS[span][1]
+            nc.sync.dma_start(tables[span][:, c0:c1], words_hbm[:, PACK * c0:PACK * c1].bitcast(I32))
 
-        picked, narrow = {}, {}
+        picked_words, picked_scales = {}, {}
 
-        def gather_words(chunk, d):
-            table, v0, v1 = chunks[chunk]
-            if chunk == "first":
-                got = keep.tile([P, P], U32, name=f"words_first_{d}", align_bytes=64)[:]
-            elif chunk == "last":
-                got = narrow["end"][:, 768 + d * P:768 + (d + 1) * P]
-            elif chunk == "mid":
-                if d == 0:
-                    narrow["end"] = keep.tile([P, 768 + D * P], U32, name="words_end", tag="scale_table", align_bytes=64)
-                got = narrow["end"][:, 256 * d:256 * (d + 1)]
-            else:
-                got = keep.tile([P, v1 - v0], U32, name=f"words_{chunk}_{d}", align_bytes=64)[:]
-            nc.vector.tensor_copy(got, tables[table][:, 0:R * v1].bitcast(U32).indirect(entries(d, v0, v1)))
-            picked[chunk, d] = got
+        def gather_words(span, d, dst):
+            nc.vector.tensor_copy(dst, tables[span][:].bitcast(U32).indirect(entries(d, *SPANS[span])))
+            picked_words[span, d] = dst
 
-        picked_scales = {}
+        def gather_words_to_own_tile(span, d):
+            v0, v1 = SPANS[span]
+            gather_words(span, d, keep.tile([P, v1 - v0], U32, name=f"words_{span}_{d}", align_bytes=64)[:])
 
-        def gather_scales(vh, d):
-            if vh == 1 or d == 0:
-                got = keep.tile([P, V // 2], U8, name=f"scales_{vh}_{d}", align_bytes=64)[:]
-            else:
-                got = keep.tile([P, V // 2], U8, name=f"scales_{vh}_{d}", tag=f"stage_1_{d}", align_bytes=64)[:]
-            v0, v1 = vh * V // 2, (vh + 1) * V // 2
-            nc.vector.tensor_copy(got, scale_table[:, 0:v1].bitcast(U8).indirect(entries(d, v0, v1)))
-            picked_scales[vh, d] = got
+        def gather_scales(v_half, d, tag):
+            v0, v1 = v_half * V_HALF, (v_half + 1) * V_HALF
+            dst = keep.tile([P, V_HALF], U8, name=f"scales_{v_half}_{d}", tag=tag, align_bytes=64)[:]
+            window = scale_table[:, 0:STRIDE * v1 // PACK].bitcast(U8)
+            nc.vector.tensor_copy(dst, window.indirect(entries(d, v0, v1)))
+            picked_scales[v_half, d] = dst
 
         raw, grouped, w_codes, w_scales = {}, {}, {}, {}
 
-        def load_w(h, d):
-            raw[h, d] = later.tile([P, PACK, HALF], F32, name=f"raw_{h}_{d}", tag=f"wide_{h}_{d}", align_bytes=64)
-            nc.sync.dma_start(raw[h, d][:], w[d].rearrange("(p t) m -> p t m", t=PACK)[:, :, h * HALF:(h + 1) * HALF])
+        def load_w(d):
+            raw[d] = later.tile([P, PACK, M], F32, name=f"raw_{d}", tag=f"raw_{d}", align_bytes=64)
+            nc.sync.dma_start(raw[d][:], w[d].rearrange("(p t) m -> p t m", t=PACK))
 
         def round_w(h, d):
-            grouped[h, d] = keep.tile([P, HALF, PACK], BF16, name=f"grouped_{h}_{d}", tag=f"stage_{h}_{d}", align_bytes=64)
+            grouped[h, d] = keep.tile([P, M_HALF, PACK], BF16, name=f"grouped_{h}_{d}", tag=f"grouped_{h}_{d}", align_bytes=64)
             nc.scalar.copy(grouped[h, d][:].rearrange("p (c i) t -> p c t i", i=2),
-                           raw[h, d][:].rearrange("p t (c i) -> p c t i", i=2))
+                           raw[d][:, :, h * M_HALF:(h + 1) * M_HALF].rearrange("p t (c i) -> p c t i", i=2))
 
         def quantize_w(h, d):
-            w_codes[h, d] = keep.tile([P, HALF], U32, name=f"w_codes_{h}_{d}", align_bytes=64)
-            w_scales[h, d] = keep.tile([P, HALF], U8, name=f"w_scales_{h}_{d}", align_bytes=64)
+            w_codes[h, d] = keep.tile([P, M_HALF], U32, name=f"w_codes_{h}_{d}", align_bytes=64)
+            w_scales[h, d] = keep.tile([P, M_HALF], U8, name=f"w_scales_{h}_{d}", align_bytes=64)
             nc.vector.quantize_mx(out=w_codes[h, d][:].bitcast(FP8X4), scales=w_scales[h, d][:],
                                   in_=grouped[h, d][:].rearrange("p m t -> p (m t)"))
 
-        def multiply(acc, c, chunk, d):
+        def multiply(acc, c, span, d):
             h, m0 = c // 2, (c % 2) * P
-            v0, v1 = chunks[chunk][1:]
-            vh = v0 // (V // 2)
-            s0 = v0 - vh * (V // 2)
+            v0, v1 = SPANS[span]
+            v_half, s0 = divmod(v0, V_HALF)
             nc.tensor.matmul_mx(out=acc, lhsT=w_codes[h, d][:, m0:m0 + P].bitcast(FP8X4), lhsT_scale=w_scales[h, d][:, m0:m0 + P],
-                                rhs=picked[chunk, d].bitcast(FP8X4), rhs_scale=picked_scales[vh, d][:, s0:s0 + v1 - v0],
-                                start=(d == 0), stop=(d == D - 1))
+                                rhs=picked_words[span, d].bitcast(FP8X4), rhs_scale=picked_scales[v_half, d][:, s0:s0 + v1 - v0],
+                                start=(d == 0), stop=(d == TAPS - 1))
 
-        def finish(dst, acc, c, on_vector):
-            if on_vector:
-                nc.vector.tensor_scalar(dst, acc, bias[:, c:c + 1], floor[:], ADD, MAX)
-            else:
-                nc.scalar.activation(dst, acc, RELU, bias=bias[:, c:c + 1])
+        def finish_on_scalar(dst, acc, c):
+            nc.scalar.activation(dst, acc, RELU, bias=bias[:, c:c + 1])
+
+        def finish_on_vector(dst, acc, c):
+            nc.vector.tensor_scalar(dst, acc, bias[:, c:c + 1], floor[:], ADD, MAX)
 
         out_rows = out.rearrange("(c p) v -> p c v", p=P)
 
+        def store(span, c0, c1, src):
+            v0, v1 = SPANS[span]
+            nc.sync.dma_start(out_rows[:, c0:c1, v0:v1], src)
+
         load_words("first")
-        for q in range(4):
-            nc.sync.dma_start(scale_table[32 * q:32 * q + 4, :], x_scales[0][4 * q:4 * q + 4, :].bitcast(I32))
-        load_w(0, 0)
+        scale_rows = x_scales[0].rearrange("(q j) c -> j q c", j=4)
+        for j in range(4):
+            nc.sync.dma_start(scale_table[j:P:QUADRANT, :], scale_rows[j].bitcast(I32))
+        load_w(0)
         load_words("high")
-        load_w(0, 1)
-        load_w(0, 2)
-        load_w(1, 0)
+        load_w(1)
+        load_w(2)
         with nc.allow_non_contiguous_dma(reason="one bias value a partition"):
             nc.sync.dma_start(bias[:], b.rearrange("(c p) o -> p (c o)", p=P))
-        load_w(1, 1)
-        load_w(1, 2)
         load_words("mid")
         load_words("last")
 
-        for h in range(2):
-            for d in range(D):
-                if (h, d) < (1, 0):
-                    round_w(h, d)
-        for d in range(D):
-            gather_words("first", d)
-        for d in range(D):
-            gather_scales(1, d)
-        for d in range(D):
-            quantize_w(0, d)
-            gather_words("high", d)
-        for d in range(D):
-            round_w(1, d)
-        gather_scales(0, 0)
+        for d in range(TAPS):
+            for h in range(2):
+                round_w(h, d)
+
+        for d in range(TAPS):
+            gather_words_to_own_tile("first", d)
+        for d in range(TAPS):
+            gather_scales(1, d, f"scales_1_{d}")
+        gather_scales(0, 0, "scales_0_0")
+        quantize_w(0, 0)
         quantize_w(1, 0)
+        for d in range(TAPS):
+            gather_words_to_own_tile("high", d)
+        quantize_w(0, 1)
         quantize_w(1, 1)
-        gather_scales(0, 1)
+        gather_scales(0, 1, "grouped_1_1")
+        quantize_w(0, 2)
+        gather_scales(0, 2, "grouped_0_2")
         quantize_w(1, 2)
-        gather_scales(0, 2)
 
-        high = [psum.tile([P, 512], F32, name=f"high_{c}", tag=f"bank{c}") for c in range(4)]
-        lower = [psum.tile([P, 512], F32, name=f"lower_{c}", tag=f"bank{4 + c}") for c in range(4)]
+        n_first, n_high, n_mid, n_last = [SPANS[span][1] - SPANS[span][0] for span in ("first", "high", "mid", "last")]
+        high = [psum.tile([P, BANK], F32, name=f"high_{c}", tag=f"bank{c}") for c in range(BLOCKS)]
+        first = [psum.tile([P, BANK], F32, name=f"first_{j}", tag=f"bank{4 + j}") for j in range(2)]
 
-        def multiply_high(h):
-            for d in range(D):
-                for c in (2 * h, 2 * h + 1):
-                    multiply(high[c][:], c, "high", d)
-
-        def store_high(h):
-            res = res_high[h]
+        early = later.tile([P, 2 * n_high + BLOCKS * n_first], F32, name="res_early", tag="raw_2", align_bytes=64)
+        res_first = early[:, 2 * n_high:].rearrange("p (c v) -> p c v", c=BLOCKS)
+        res_high = [early[:, 0:2 * n_high].rearrange("p (c v) -> p c v", c=2), keep.tile([P, 2, n_high], F32, name="res_high_1")[:]]
+        for d in range(TAPS):
+            for c in range(BLOCKS):
+                multiply(high[c][:], c, "high", d)
             for j in range(2):
-                finish(res[:, j, :], high[2 * h + j][:], 2 * h + j, False)
-            nc.sync.dma_start(out_rows[:, 2 * h:2 * h + 2, 512:1024], res)
-
-        early = later.tile([P, 2 * 512 + 4 * 128], F32, name="res_early", tag="wide_1_2", align_bytes=64)
-        res_first = early[:, 1024:].rearrange("p (c v) -> p c v", c=4)
-        res_high = [early[:, 0:1024].rearrange("p (c v) -> p c v", c=2), keep.tile([P, 2, 512], F32, name="res_high_1")[:]]
-        for h in range(2):
-            multiply_high(h)
-            store_high(h)
-        first = [psum.tile([P, 512], F32, name=f"first_{h}", tag=f"bank{h}") for h in range(2)]
-        for j in range(2):
-            for d in range(D):
-                for h in range(2):
-                    multiply(first[h][:, j * P:(j + 1) * P], 2 * h + j, "first", d)
-        for c in range(4):
-            finish(res_first[:, c, :], first[c // 2][:, (c % 2) * P:(c % 2 + 1) * P], c, False)
-        nc.sync.dma_start(out_rows[:, :, 128:256], res_first)
-
-        for d in range(D):
-            gather_words("mid", d)
-        for d in range(D):
-            for c in range(4):
-                multiply(lower[c][:, 0:256], c, "mid", d)
-        for d in range(D):
-            gather_words("last", d)
-        for h in range(2):
-            res = keep.tile([P, 2, 256], F32, name=f"res_mid_{h}")
+                multiply(first[j][:, 0:n_first], j, "first", d)
+        for d in range(TAPS):
             for j in range(2):
-                finish(res[:, j, :], lower[2 * h + j][:, 0:256], 2 * h + j, False)
-            nc.sync.dma_start(out_rows[:, 2 * h:2 * h + 2, 256:512], res[:])
+                multiply(first[j][:, n_first:2 * n_first], 2 + j, "first", d)
+        for c in range(BLOCKS):
+            h, j = divmod(c, 2)
+            finish_on_scalar(res_high[h][:, j, :], high[c][:], c)
+            store("high", c, c + 1, res_high[h][:, j:j + 1, :])
+        for c in range(BLOCKS):
+            h, j = divmod(c, 2)
+            finish_on_scalar(res_first[:, c, :], first[j][:, h * n_first:(h + 1) * n_first], c)
+        store("first", 0, BLOCKS, res_first)
 
-        last = [psum.tile([P, 512], F32, name=f"last_{c}", tag=f"bank{c}") for c in range(4)]
-        for d in range(D):
-            for c in range(4):
-                multiply(last[c][:, 0:128], c, "last", d)
-        res_last = keep.tile([P, 4, 128], F32, name="res_last")
-        for c in range(4):
-            finish(res_last[:, c, :], last[c][:, 0:128], c, True)
-            if c % 2:
-                nc.sync.dma_start(out_rows[:, c - 1:c + 1, 0:128], res_last[:, c - 1:c + 1, :])
+        mid = [psum.tile([P, BANK], F32, name=f"mid_{c}", tag=f"bank{(6 + c) % 8}") for c in range(BLOCKS)]
+        words_end = keep.tile([P, TAPS * (n_mid + n_last)], U32, name="words_end", tag="grouped_1_2", align_bytes=64)
+        for d in range(TAPS):
+            gather_words("mid", d, words_end[:, d * n_mid:(d + 1) * n_mid])
+        for d in range(TAPS):
+            for c in range(BLOCKS):
+                multiply(mid[c][:, 0:n_mid], c, "mid", d)
+        for d in range(TAPS):
+            gather_words("last", d, words_end[:, TAPS * n_mid + d * n_last:TAPS * n_mid + (d + 1) * n_last])
+        for h in range(2):
+            res_mid = keep.tile([P, 2, n_mid], F32, name=f"res_mid_{h}")
+            for j in range(2):
+                finish_on_scalar(res_mid[:, j, :], mid[2 * h + j][:, 0:n_mid], 2 * h + j)
+            store("mid", 2 * h, 2 * h + 2, res_mid[:])
+
+        last = [psum.tile([P, BANK], F32, name=f"last_{c}", tag=f"bank{2 + c}") for c in range(BLOCKS)]
+        for d in range(TAPS):
+            for c in range(BLOCKS):
+                multiply(last[c][:, 0:n_last], c, "last", d)
+        res_last = keep.tile([P, BLOCKS, n_last], F32, name="res_last")
+        for h in range(2):
+            for c in (2 * h, 2 * h + 1):
+                finish_on_vector(res_last[:, c, :], last[c][:, 0:n_last], c)
+            store("last", 2 * h, 2 * h + 2, res_last[:, 2 * h:2 * h + 2, :])

from contextlib import ExitStack

import concourse.mybir as mybir

K, T, TAPS, V, STRIDE, M = 512, 4096, 3, 1024, 4, 512
FLOPS = 2 * K * M * TAPS * V

F32 = mybir.dt.float32
BF16 = mybir.dt.bfloat16
I32 = mybir.dt.int32
U32 = mybir.dt.uint32
U16 = mybir.dt.uint16
U8 = mybir.dt.uint8
FP8X4 = mybir.dt.float8_e4m3fn_x4
RELU = mybir.ActivationFunctionType.Relu
ADD = mybir.AluOpType.add
MAX = mybir.AluOpType.max

P = 128
PACK = 4
BLOCKS = M // P
M_HALF = M // 2
V_HALF = V // 2
BANK = 512
QUADRANT = 32
HEAD_WORDS = 16384

SPANS = {"first": (128, 256), "high": (512, 1024), "mid": (256, 512), "last": (0, 128)}


def tile_picked_deform_lin_relu_def_p_kernel(tc, x_words, x_scales, w, b, offs, out):
    nc = tc.nc
    with ExitStack() as ctx:
        keep = ctx.enter_context(tc.tile_pool(name="keep", bufs=1))
        psum = ctx.enter_context(tc.psum_pool(name="psum", bufs=1))

        offsets = keep.tile([P, TAPS * V // 16], U16, name="offsets")
        nc.sync.dma_start(offsets[:], offs)

        def entries(d, v0, v1):
            return offsets[:, (d * V + v0) // 16:(d * V + v1) // 16]

        scale_table = keep.tile([P, T // PACK], I32, name="scale_table", align_bytes=64)
        nc.vector.memset(scale_table[:], 0)

        floor = keep.tile([P, 1], F32, name="floor")
        with tc.tile_pool(name="head", bufs=1) as head:
            zero = head.tile([P, HEAD_WORDS], F32, name="zero")
            nc.vector.memset(zero[:, 0:1], 0.0)
            nc.scalar.activation(floor[:], zero[:, 0:1], RELU)
        later = ctx.enter_context(tc.tile_pool(name="later", bufs=1))
        bias = later.tile([P, BLOCKS], F32, name="bias")

        words_hbm = x_words[0].rearrange("p c r -> p (c r)")
        tables = {}
        for span in ("high", "mid", "first", "last"):
            pool = keep if span == "first" else later
            tables[span] = pool.tile([P, STRIDE * SPANS[span][1]], I32, name=f"table_{span}", align_bytes=64)

        def load_words(span):
            c0, c1 = STRIDE * SPANS[span][0], STRIDE * SPANS[span][1]
            nc.sync.dma_start(tables[span][:, c0:c1], words_hbm[:, PACK * c0:PACK * c1].bitcast(I32))

        picked_words, picked_scales = {}, {}

        def gather_words(span, d, dst):
            nc.vector.tensor_copy(dst, tables[span][:].bitcast(U32).indirect(entries(d, *SPANS[span])))
            picked_words[span, d] = dst

        def gather_words_to_own_tile(span, d):
            v0, v1 = SPANS[span]
            gather_words(span, d, keep.tile([P, v1 - v0], U32, name=f"words_{span}_{d}", align_bytes=64)[:])

        def gather_scales(v_half, d, tag):
            v0, v1 = v_half * V_HALF, (v_half + 1) * V_HALF
            dst = keep.tile([P, V_HALF], U8, name=f"scales_{v_half}_{d}", tag=tag, align_bytes=64)[:]
            window = scale_table[:, 0:STRIDE * v1 // PACK].bitcast(U8)
            nc.vector.tensor_copy(dst, window.indirect(entries(d, v0, v1)))
            picked_scales[v_half, d] = dst

        raw, grouped, w_codes, w_scales = {}, {}, {}, {}

        def load_w(d):
            raw[d] = later.tile([P, PACK, M], F32, name=f"raw_{d}", tag=f"raw_{d}", align_bytes=64)
            nc.sync.dma_start(raw[d][:], w[d].rearrange("(p t) m -> p t m", t=PACK))

        def round_w(h, d):
            grouped[h, d] = keep.tile([P, M_HALF, PACK], BF16, name=f"grouped_{h}_{d}", tag=f"grouped_{h}_{d}", align_bytes=64)
            nc.scalar.copy(grouped[h, d][:].rearrange("p (c i) t -> p c t i", i=2),
                           raw[d][:, :, h * M_HALF:(h + 1) * M_HALF].rearrange("p t (c i) -> p c t i", i=2))

        def quantize_w(h, d):
            w_codes[h, d] = keep.tile([P, M_HALF], U32, name=f"w_codes_{h}_{d}", align_bytes=64)
            w_scales[h, d] = keep.tile([P, M_HALF], U8, name=f"w_scales_{h}_{d}", align_bytes=64)
            nc.vector.quantize_mx(out=w_codes[h, d][:].bitcast(FP8X4), scales=w_scales[h, d][:],
                                  in_=grouped[h, d][:].rearrange("p m t -> p (m t)"))

        def multiply(acc, c, span, d):
            h, m0 = c // 2, (c % 2) * P
            v0, v1 = SPANS[span]
            v_half, s0 = divmod(v0, V_HALF)
            nc.tensor.matmul_mx(out=acc, lhsT=w_codes[h, d][:, m0:m0 + P].bitcast(FP8X4), lhsT_scale=w_scales[h, d][:, m0:m0 + P],
                                rhs=picked_words[span, d].bitcast(FP8X4), rhs_scale=picked_scales[v_half, d][:, s0:s0 + v1 - v0],
                                start=(d == 0), stop=(d == TAPS - 1))

        def finish_on_scalar(dst, acc, c):
            nc.scalar.activation(dst, acc, RELU, bias=bias[:, c:c + 1])

        def finish_on_vector(dst, acc, c):
            nc.vector.tensor_scalar(dst, acc, bias[:, c:c + 1], floor[:], ADD, MAX)

        out_rows = out.rearrange("(c p) v -> p c v", p=P)

        def store(span, c0, c1, src):
            v0, v1 = SPANS[span]
            nc.sync.dma_start(out_rows[:, c0:c1, v0:v1], src)

        load_words("first")
        scale_rows = x_scales[0].rearrange("(q j) c -> j q c", j=4)
        for j in range(4):
            nc.sync.dma_start(scale_table[j:P:QUADRANT, :], scale_rows[j].bitcast(I32))
        load_w(0)
        load_words("high")
        load_w(1)
        load_w(2)
        with nc.allow_non_contiguous_dma(reason="one bias value a partition"):
            nc.sync.dma_start(bias[:], b.rearrange("(c p) o -> p (c o)", p=P))
        load_words("mid")
        load_words("last")

        for d in range(TAPS):
            for h in range(2):
                round_w(h, d)

        for d in range(TAPS):
            gather_words_to_own_tile("first", d)
        for d in range(TAPS):
            gather_scales(1, d, f"scales_1_{d}")
        gather_scales(0, 0, "scales_0_0")
        quantize_w(0, 0)
        quantize_w(1, 0)
        for d in range(TAPS):
            gather_words_to_own_tile("high", d)
        quantize_w(0, 1)
        quantize_w(1, 1)
        gather_scales(0, 1, "grouped_1_1")
        quantize_w(0, 2)
        gather_scales(0, 2, "grouped_0_2")
        quantize_w(1, 2)

        n_first, n_high, n_mid, n_last = [SPANS[span][1] - SPANS[span][0] for span in ("first", "high", "mid", "last")]
        high = [psum.tile([P, BANK], F32, name=f"high_{c}", tag=f"bank{c}") for c in range(BLOCKS)]
        first = [psum.tile([P, BANK], F32, name=f"first_{j}", tag=f"bank{4 + j}") for j in range(2)]

        early = later.tile([P, 2 * n_high + BLOCKS * n_first], F32, name="res_early", tag="raw_2", align_bytes=64)
        res_first = early[:, 2 * n_high:].rearrange("p (c v) -> p c v", c=BLOCKS)
        res_high = [early[:, 0:2 * n_high].rearrange("p (c v) -> p c v", c=2), keep.tile([P, 2, n_high], F32, name="res_high_1")[:]]
        for d in range(TAPS):
            for c in range(BLOCKS):
                multiply(high[c][:], c, "high", d)
            for j in range(2):
                multiply(first[j][:, 0:n_first], j, "first", d)
        for d in range(TAPS):
            for j in range(2):
                multiply(first[j][:, n_first:2 * n_first], 2 + j, "first", d)
        for c in range(BLOCKS):
            h, j = divmod(c, 2)
            finish_on_scalar(res_high[h][:, j, :], high[c][:], c)
            store("high", c, c + 1, res_high[h][:, j:j + 1, :])
        for c in range(BLOCKS):
            h, j = divmod(c, 2)
            finish_on_scalar(res_first[:, c, :], first[j][:, h * n_first:(h + 1) * n_first], c)
        store("first", 0, BLOCKS, res_first)

        mid = [psum.tile([P, BANK], F32, name=f"mid_{c}", tag=f"bank{(6 + c) % 8}") for c in range(BLOCKS)]
        words_end = keep.tile([P, TAPS * (n_mid + n_last)], U32, name="words_end", tag="grouped_1_2", align_bytes=64)
        for d in range(TAPS):
            gather_words("mid", d, words_end[:, d * n_mid:(d + 1) * n_mid])
        for d in range(TAPS):
            for c in range(BLOCKS):
                multiply(mid[c][:, 0:n_mid], c, "mid", d)
        for d in range(TAPS):
            gather_words("last", d, words_end[:, TAPS * n_mid + d * n_last:TAPS * n_mid + (d + 1) * n_last])
        for h in range(2):
            res_mid = keep.tile([P, 2, n_mid], F32, name=f"res_mid_{h}")
            for j in range(2):
                finish_on_scalar(res_mid[:, j, :], mid[2 * h + j][:, 0:n_mid], 2 * h + j)
            store("mid", 2 * h, 2 * h + 2, res_mid[:])

        last = [psum.tile([P, BANK], F32, name=f"last_{c}", tag=f"bank{2 + c}") for c in range(BLOCKS)]
        for d in range(TAPS):
            for c in range(BLOCKS):
                multiply(last[c][:, 0:n_last], c, "last", d)
        res_last = keep.tile([P, BLOCKS, n_last], F32, name="res_last")
        for h in range(2):
            for c in (2 * h, 2 * h + 1):
                finish_on_vector(res_last[:, c, :], last[c][:, 0:n_last], c)
            store("last", 2 * h, 2 * h + 2, res_last[:, 2 * h:2 * h + 2, :])
